import numpy as np
import ml_dtypes


def mxq(x, axis, fmt="e4m3"):
    dtype, down = {"e4m3": (ml_dtypes.float8_e4m3fn, 7), "e5m2": (ml_dtypes.float8_e5m2, 14)}[fmt]
    v = np.moveaxis(np.asarray(x, np.float32).astype(ml_dtypes.bfloat16).astype(np.float64), axis, -1)
    blocks = v.reshape(v.shape[:-1] + (-1, 32))
    amax = np.abs(blocks).max(-1, keepdims=True)
    byte = np.maximum(np.where(amax > 0, np.frexp(amax)[1] - 1 + 127, 0) - down, 1)
    scale = np.exp2(byte - 127.0)
    codes = (blocks / scale).astype(np.float32).astype(dtype).astype(np.float64)
    return np.moveaxis((codes * scale).reshape(v.shape), -1, axis)


WIDE = False


def mx_kscale(k):
    if not WIDE:
        return np.ones(k)
    levels = np.array([10, -10, 5, -5, 0])
    if k % 512:
        return np.exp2(np.random.permutation(np.resize(levels, k // 32))).repeat(32)
    a = np.empty((k // 512, 16))
    for p in range(k // 512):
        a[p, :8] = np.random.permutation(np.resize(levels, 8))
        for g in range(8):
            far = levels[np.abs(levels - a[p, g]) >= 10]
            a[p, g + 8] = far[np.random.randint(len(far))]
    return np.exp2(a.ravel()).repeat(32)


def f64(x):
    return np.asarray(x).astype(np.float64)


def striped(idx):
    return np.tile(idx.reshape(-1, 16).T, (8, 1)).astype(np.uint16)


def unstriped(offs):
    return offs[:16].T.reshape(-1).astype(np.int64)


def pack_weight(w):
    k, n = w.shape
    w = f64(np.asarray(w, np.float32).astype(ml_dtypes.bfloat16)).reshape(k // 32, 32, n)
    amax = np.abs(w).max(1)
    byte = np.clip(np.where(amax > 0, np.frexp(amax)[1] - 1 + 127 - 7, 1), 1, 254)
    scaled = (w * np.exp2(127.0 - byte)[:, None, :]).reshape(k, n).astype(np.float32)
    words = np.ascontiguousarray(scaled.reshape(k // 512, 128, 4, n).transpose(0, 1, 3, 2)).astype(ml_dtypes.float8_e4m3fn).view(np.uint8)
    return words, np.ascontiguousarray(byte.astype(np.uint8).reshape(k // 512, 16, n))


def unpack_weight(words, scales):
    g, p, n, _ = words.shape
    vals = np.ascontiguousarray(words).view(ml_dtypes.float8_e4m3fn).astype(np.float64) * np.repeat(np.exp2(scales.astype(np.float64) - 127.0), 8, axis=1)[..., None]
    return vals.transpose(0, 1, 3, 2).reshape(g * 512, n)


K, T, S, N, U, D, V = 1024, 1024, 256, 128, 1024, 4, 256
P = 2 ** 7


def setup_inputs():
    n = np.random.standard_normal
    s = mx_kscale(K)[:, None]
    packed_xT = pack_weight(n((K, T)) * s)
    return {
        "x_words": packed_xT[0],
        "x_scales": packed_xT[1],
        "w1": (n((K, N)) / np.sqrt(K) / s).astype(np.float32),
        "w2": (n((K, N)) / np.sqrt(K) / s).astype(np.float32),
        "w3": (n((K, N)) / np.sqrt(K) / s).astype(np.float32),
        "time": (np.tile(np.random.uniform(0.3, 4.0, U), (P, 1))).astype(np.float32),
        "lam": (np.random.uniform(0.4, 1.2, (N, 1))).astype(np.float32),
        "cash": (np.tile(np.random.uniform(0.2, 1.5, U), (P, 1))).astype(np.float32),
        "offs": striped(np.random.permutation(T)[:S]),
        "iss": striped(np.repeat(np.random.permutation(S)[:V], D)),
    }


def reference(x_words, x_scales, w1, w2, w3, time, lam, cash, offs, iss):
    xq = unpack_weight(x_words, x_scales)[:, unstriped(offs)]
    yl = mxq(f64(w1), 0, "e4m3").T @ xq
    lg = yl[:, unstriped(iss)]
    ys = mxq(f64(w2), 0, "e4m3").T @ xq
    sl = ys[:, unstriped(iss)]
    dk = np.exp(-1.0 * (f64(lam) * f64(time)[:1]))
    ld = (-1.0 * dk + 1.0) / (f64(lam) * f64(time)[:1])
    yh = mxq(f64(w3), 0, "e4m3").T @ xq
    hp = yh[:, unstriped(iss)]
    yld = 0.15 * (lg + 1.5) + 0.3 * (sl * ld + hp * (ld - dk))
    df = np.exp(-1.0 * (yld * f64(time)[:1]))
    pv = f64(cash)[:1] * df
    return pv.reshape(len(pv), -1, D).sum(axis=2)

@@ -1,0 +1,228 @@
+from contextlib import ExitStack
+
+import concourse.mybir as mybir
+from concourse.masks import make_identity
+
+K, T, S, M, R, D = 1024, 1024, 256, 128, 1024, 4
+FLOPS = 3 * 2 * K * M * S
+
+F32 = mybir.dt.float32
+BF16 = mybir.dt.bfloat16
+I32 = mybir.dt.int32
+U32 = mybir.dt.uint32
+U16 = mybir.dt.uint16
+U8 = mybir.dt.uint8
+FP8X4 = mybir.dt.float8_e4m3fn_x4
+ALU = mybir.AluOpType
+ACT = mybir.ActivationFunctionType
+
+P = 128
+PACK = 4
+PASSES = K // (P * PACK)
+BANK = 512
+BLOCKS = R // P
+CHUNK = 256
+CHUNKS = R // CHUNK
+WINDOW = CHUNK + 16
+LAM_ROW = 15
+TIME_ROW = 16
+CASH_ROW = 24
+
+
+def interleave(engine_copy, grouped, raw):
+    engine_copy(
+        out=grouped.rearrange("p (c i) j -> p c j i", i=4),
+        in_=raw.rearrange("p j (c i) -> p c j i", i=4),
+    )
+
+
+def tile_picked_ynels_price_p_kernel(
+    tc, x_words, x_scales, w1, w2, w3, time, lam, cash, offs, iss, out
+):
+    nc = tc.nc
+    with ExitStack() as ctx:
+        sb = ctx.enter_context(tc.tile_pool(name="sb", bufs=1))
+        ps = ctx.enter_context(tc.psum_pool(name="ps", bufs=1))
+
+        def bank(i, cols, name):
+            return ps.tile([P, cols], F32, name=name, tag="bank%d" % i)
+
+        rows = sb.tile([P, P], F32, name="rows", tag="rows")
+        scale_win = sb.tile([P, T], U8, name="scale_win", align_bytes=64)
+        nc.vector.memset(scale_win[:].bitcast(I32), 0)
+        for lo, hi in ((0, LAM_ROW), (32, 64), (64, P)):
+            nc.vector.memset(rows[lo:hi, :], 0.0)
+        ident = sb.tile([P, P], F32, name="ident")
+        make_identity(nc, ident[:])
+
+        nc.scalar.dma_start(out=rows[TIME_ROW : TIME_ROW + BLOCKS, :], in_=time[0].rearrange("(b n) -> b n", n=P))
+        nc.scalar.dma_start(out=rows[LAM_ROW : LAM_ROW + 1, :], in_=lam.rearrange("m o -> o m"))
+        nc.scalar.dma_start(out=rows[CASH_ROW : CASH_ROW + BLOCKS, :], in_=cash[0].rearrange("(b n) -> b n", n=P))
+        for q in range(4):
+            nc.gpsimd.dma_start(
+                out=scale_win[32 * q : 32 * q + 4 * PASSES, :].bitcast(I32),
+                in_=x_scales[:, 4 * q : 4 * q + 4, :].bitcast(I32),
+            )
+
+        offs_t = sb.tile([P, S // 16], U16, name="offs_t")
+        iss_t = sb.tile([P, R // 16], U16, name="iss_t")
+        nc.sync.dma_start(offs_t[:], offs)
+
+        def load_w(w, g, name, tag):
+            raw = sb.tile([P, PACK, M], F32, name=name, tag=tag)
+            nc.sync.dma_start(out=raw[:], in_=w[512 * g : 512 * (g + 1), :].rearrange("(p j) m -> p j m", j=PACK))
+            return raw
+
+        def load_w_whole(w, name):
+            raw = sb.tile([P, PASSES, PACK, M], F32, name=name, tag=name)
+            nc.sync.dma_start(
+                out=raw[:].rearrange("p g j m -> p g (j m)"),
+                in_=w.rearrange("(g p j) m -> p g (j m)", g=PASSES, j=PACK),
+            )
+            return [raw[:, g, :, :] for g in range(PASSES)]
+
+        raw1 = load_w_whole(w1, "raw1")
+        word_win = []
+        for g in range(PASSES):
+            win = sb.tile([P, T], U32, name="word_win%d" % g, align_bytes=64)
+            nc.sync.dma_start(out=win[:].bitcast(I32), in_=x_words[g].rearrange("p n t -> p (n t)").bitcast(I32))
+            word_win.append(win)
+        nc.sync.dma_start(iss_t[:], iss)
+        raw3 = load_w_whole(w3, "raw3")
+
+        level = sb.tile([P, WINDOW], F32, name="level")
+        hump = sb.tile([P, WINDOW], F32, name="hump")
+        slope = sb.tile([P, WINDOW], F32, name="slope")
+        zeros = sb.tile([P, WINDOW - S], F32, name="zeros")
+        nc.vector.memset(zeros[:], 0.0)
+        nc.scalar.activation(out=level[:, S:], in_=zeros[:], func=ACT.Exp)
+        nc.vector.memset(hump[:, S:], 0.0)
+        nc.vector.memset(slope[:, S:], 0.0)
+
+        rows_t = bank(0, P, "rows_t")
+        nc.tensor.transpose(rows_t[:], rows[:], ident[:])
+        cols = sb.tile([P, 2 * BLOCKS], F32, name="cols")
+        nc.vector.tensor_copy(out=cols[:], in_=rows_t[:, TIME_ROW : TIME_ROW + 2 * BLOCKS])
+        neg_lam = sb.tile([P, 1], F32, name="neg_lam")
+        nc.vector.tensor_scalar(out=neg_lam[:], in0=rows_t[:, LAM_ROW : LAM_ROW + 1], scalar1=-1.0, scalar2=None, op0=ALU.mult)
+        recips = sb.tile([P, BLOCKS + 1], F32, name="recips")
+        nc.vector.reciprocal(out=recips[:], in_=rows_t[:, LAM_ROW : LAM_ROW + BLOCKS + 1])
+        kappa = sb.tile([P, 1], F32, name="kappa")
+        nc.vector.tensor_scalar(out=kappa[:], in0=recips[:, 0:1], scalar1=0.3, scalar2=None, op0=ALU.mult)
+
+        def spread(src, h, bank_i, name):
+            wide = bank(bank_i, BANK, name)
+            for b in range(4):
+                col = 4 * h + b
+                nc.tensor.transpose(wide[:, P * b : P * (b + 1)], src[:, col : col + 1].to_broadcast([P, P]), ident[:])
+            return wide
+
+        decay = sb.tile([P, R], F32, name="decay")
+        load = sb.tile([P, R], F32, name="load")
+        inv_wide = []
+        for h in range(2):
+            t_wide = spread(cols[:], h, 1 + h, "t_wide%d" % h)
+            nc.scalar.activation(out=decay[:, BANK * h : BANK * (h + 1)], in_=t_wide[:], func=ACT.Exp, scale=neg_lam[:])
+        for h in range(2):
+            inv_wide.append(spread(recips[:, 1:], h, 3 + h, "inv_wide%d" % h))
+
+        def quantise(raw, copies, name, split):
+            grouped = sb.tile([P, PASSES, M, PACK], BF16, name=name + "_bf", align_bytes=64)
+            codes = sb.tile([P, PASSES * M], U32, name=name + "_codes", align_bytes=64)
+            scales = sb.tile([P, PASSES * M], U8, name=name + "_scales", align_bytes=64)
+            for g in range(PASSES):
+                interleave(copies[g], grouped[:, g, :, :], raw[g])
+                if split:
+                    nc.vector.quantize_mx(
+                        out=codes[:, M * g : M * (g + 1)].bitcast(FP8X4),
+                        scales=scales[:, M * g : M * (g + 1)],
+                        in_=grouped[:, g, :, :].rearrange("p m j -> p (m j)"),
+                    )
+            if not split:
+                nc.vector.quantize_mx(
+                    out=codes[:].bitcast(FP8X4), scales=scales[:], in_=grouped[:].rearrange("p g m j -> p (g m j)")
+                )
+            return codes, scales
+
+        q1 = quantise(raw1, [nc.vector.tensor_copy] * 2, "w1", False)
+
+        x_scale = sb.tile([P, S], U8, name="x_scale", align_bytes=64)
+        nc.vector.tensor_copy(x_scale[:], scale_win[:].indirect(offs_t[:]))
+        x_code = []
+        for g in range(PASSES):
+            picked = sb.tile([P, S], U32, name="x_code%d" % g, align_bytes=64)
+            nc.vector.tensor_copy(picked[:], word_win[g][:].indirect(offs_t[:]))
+            x_code.append(picked)
+
+        def product(q, bank_i, name):
+            codes, scales = q
+            acc = bank(bank_i, S, name)
+            for g in range(PASSES):
+                nc.tensor.matmul_mx(
+                    out=acc[:],
+                    lhsT=codes[:, M * g : M * (g + 1)].bitcast(FP8X4),
+                    lhsT_scale=scales[:, M * g : M * (g + 1)],
+                    rhs=x_code[g][:].bitcast(FP8X4),
+                    rhs_scale=x_scale[4 * g : P, :],
+                    start=(g == 0),
+                    stop=(g == PASSES - 1),
+                )
+            return acc
+
+        yl = product(q1, 5, "yl")
+        nc.scalar.activation(out=level[:, 0:S], in_=yl[:], func=ACT.Copy, scale=-0.15, bias=-0.225)
+
+        for h in range(2):
+            half = slice(BANK * h, BANK * (h + 1))
+            nc.vector.scalar_tensor_tensor(
+                out=load[:, half], in0=decay[:, half], scalar=1.0, in1=inv_wide[h][:], op0=ALU.subtract, op1=ALU.mult
+            )
+
+        def offsets(c):
+            return iss_t[:, (CHUNK // 16) * c : (CHUNK // 16) * (c + 1)]
+
+        term_l = []
+        for c in range(CHUNKS):
+            term = sb.tile([P, CHUNK], F32, name="term_l%d" % c)
+            nc.vector.tensor_copy(term[:], level[:].indirect(offsets(c)))
+            term_l.append(term)
+
+        q3 = quantise(raw3, [nc.scalar.copy] * 2, "w3", False)
+        yh = product(q3, 6, "yh")
+        nc.scalar.activation(out=hump[:, 0:S], in_=yh[:], func=ACT.Copy, scale=0.3)
+        hump_k = sb.tile([P, S], F32, name="hump_k")
+        nc.scalar.activation(out=hump_k[:], in_=yh[:], func=ACT.Copy, scale=kappa[:])
+
+        raw2 = [load_w(w2, g, "raw2_%d" % g, ("rows", "raw1")[g])[:] for g in range(PASSES)]
+        q2 = quantise(raw2, [nc.scalar.copy] * 2, "w2", True)
+        ys = product(q2, 7, "ys")
+        nc.vector.scalar_tensor_tensor(
+            out=slope[:, 0:S], in0=ys[:], scalar=kappa[:], in1=hump_k[:], op0=ALU.mult, op1=ALU.add
+        )
+
+        for c in range(CHUNKS):
+            span = slice(CHUNK * c, CHUNK * (c + 1))
+            term_h = sb.tile([P, CHUNK], F32, name="term_h%d" % c)
+            nc.vector.tensor_tensor(term_h[:], hump[:].indirect(offsets(c)), decay[:, span], ALU.mult)
+            term_s = sb.tile([P, CHUNK], F32, name="term_s%d" % c)
+            nc.vector.tensor_tensor(term_s[:], slope[:].indirect(offsets(c)), load[:, span], ALU.mult)
+            back = bank(4 + c % 2, CHUNK, "back%d" % c)
+            for i in range(CHUNK // P):
+                b = c * (CHUNK // P) + i
+                part = slice(P * i, P * (i + 1))
+                total = bank(b % 4, P, "total%d" % b)
+                terms = (term_l[c], term_h, term_s)
+                for n, term in enumerate(terms):
+                    nc.tensor.matmul(
+                        total[:], lhsT=term[:, part], rhs=ident[:], start=(n == 0), stop=(n == len(terms) - 1), is_transpose=True
+                    )
+                disc = sb.tile([P, P], F32, name="disc%d" % b)
+                nc.scalar.activation(out=disc[:], in_=total[:], func=ACT.Exp, scale=cols[:, b : b + 1])
+                value = sb.tile([P, P], F32, name="value%d" % b)
+                nc.scalar.activation(out=value[:], in_=disc[:], func=ACT.Copy, scale=cols[:, BLOCKS + b : BLOCKS + b + 1])
+                nc.tensor.transpose(back[:, part], value[:], ident[:])
+            price = sb.tile([P, CHUNK // D], F32, name="price%d" % c)
+            nc.vector.tensor_reduce(
+                out=price[:], in_=back[:].rearrange("p (v d) -> p v d", d=D), axis=mybir.AxisListType.X, op=ALU.add
+            )
+            nc.sync.dma_start(out=out[:, (CHUNK // D) * c : (CHUNK // D) * (c + 1)], in_=price[:])

@@ -23,10 +23,9 @@ BANK = 512
 BLOCKS = R // P
 CHUNK = 256
 CHUNKS = R // CHUNK
-WINDOW = CHUNK + 16
-LAM_ROW = 15
-TIME_ROW = 16
-CASH_ROW = 24
+HALF = 512
+SPARE = 16
+RUN = R // P
 
 
 def interleave(engine_copy, grouped, raw):
@@ -47,112 +46,113 @@ def tile_picked_ynels_price_p_kernel(
         def bank(i, cols, name):
             return ps.tile([P, cols], F32, name=name, tag="bank%d" % i)
 
-        rows = sb.tile([P, P], F32, name="rows", tag="rows")
         scale_win = sb.tile([P, T], U8, name="scale_win", align_bytes=64)
-        nc.vector.memset(scale_win[:].bitcast(I32), 0)
-        for lo, hi in ((0, LAM_ROW), (32, 64), (64, P)):
-            nc.vector.memset(rows[lo:hi, :], 0.0)
+        nc.gpsimd.memset(scale_win[:].bitcast(I32), 0)
         ident = sb.tile([P, P], F32, name="ident")
         make_identity(nc, ident[:])
+        level = sb.tile([P, CHUNK + SPARE], F32, name="level")
+        hump = sb.tile([P, HALF + SPARE], F32, name="hump")
+        slope = sb.tile([P, HALF + SPARE], F32, name="slope")
+        nc.vector.memset(hump[:, S:], 0.0)
+        nc.vector.memset(slope[:, S:], 0.0)
+        rows = sb.tile([P, CHUNK], F32, name="rows")
+        nc.vector.memset(rows[:], 0.0)
 
-        nc.scalar.dma_start(out=rows[TIME_ROW : TIME_ROW + BLOCKS, :], in_=time[0].rearrange("(b n) -> b n", n=P))
-        nc.scalar.dma_start(out=rows[LAM_ROW : LAM_ROW + 1, :], in_=lam.rearrange("m o -> o m"))
-        nc.scalar.dma_start(out=rows[CASH_ROW : CASH_ROW + BLOCKS, :], in_=cash[0].rearrange("(b n) -> b n", n=P))
-        for q in range(4):
-            nc.gpsimd.dma_start(
-                out=scale_win[32 * q : 32 * q + 4 * PASSES, :].bitcast(I32),
-                in_=x_scales[:, 4 * q : 4 * q + 4, :].bitcast(I32),
-            )
+        nc.scalar.activation(out=level[:, S:], in_=hump[:, S : S + SPARE], func=ACT.Exp)
 
         offs_t = sb.tile([P, S // 16], U16, name="offs_t")
         iss_t = sb.tile([P, R // 16], U16, name="iss_t")
-        nc.sync.dma_start(offs_t[:], offs)
-
-        def load_w(w, g, name, tag):
-            raw = sb.tile([P, PACK, M], F32, name=name, tag=tag)
-            nc.sync.dma_start(out=raw[:], in_=w[512 * g : 512 * (g + 1), :].rearrange("(p j) m -> p j m", j=PACK))
-            return raw
 
         def load_w_whole(w, name):
-            raw = sb.tile([P, PASSES, PACK, M], F32, name=name, tag=name)
+            raw = sb.tile([P, PASSES, PACK, M], F32, name=name)
             nc.sync.dma_start(
                 out=raw[:].rearrange("p g j m -> p g (j m)"),
                 in_=w.rearrange("(g p j) m -> p g (j m)", g=PASSES, j=PACK),
             )
             return [raw[:, g, :, :] for g in range(PASSES)]
 
-        raw1 = load_w_whole(w1, "raw1")
-        word_win = []
-        for g in range(PASSES):
-            win = sb.tile([P, T], U32, name="word_win%d" % g, align_bytes=64)
-            nc.sync.dma_start(out=win[:].bitcast(I32), in_=x_words[g].rearrange("p n t -> p (n t)").bitcast(I32))
-            word_win.append(win)
-        nc.sync.dma_start(iss_t[:], iss)
+        small = sb.tile([P, 2, 4], F32, name="small")
+        nc.sync.dma_start(out=small[:], in_=time[0].rearrange("(h p j) -> p h j", h=2, j=4))
+        nc.sync.dma_start(offs_t[:], offs)
         raw3 = load_w_whole(w3, "raw3")
+        lam_col = sb.tile([P, 1], F32, name="lam_col")
+        nc.sync.dma_start(out=lam_col[:], in_=lam)
+        def load_words(g):
+            win = sb.tile([P, T], U32, name="word_win%d" % g, tag="word_win%d" % g, align_bytes=64)
+            nc.sync.dma_start(out=win[:].bitcast(I32), in_=x_words[g].rearrange("p n t -> p (n t)").bitcast(I32))
+            return win
 
-        level = sb.tile([P, WINDOW], F32, name="level")
-        hump = sb.tile([P, WINDOW], F32, name="hump")
-        slope = sb.tile([P, WINDOW], F32, name="slope")
-        zeros = sb.tile([P, WINDOW - S], F32, name="zeros")
-        nc.vector.memset(zeros[:], 0.0)
-        nc.scalar.activation(out=level[:, S:], in_=zeros[:], func=ACT.Exp)
-        nc.vector.memset(hump[:, S:], 0.0)
-        nc.vector.memset(slope[:, S:], 0.0)
+        word_win = [load_words(0)]
+        for q in range(4):
+            nc.sync.dma_start(
+                out=scale_win[32 * q : 32 * q + 4 * PASSES, :].bitcast(I32),
+                in_=x_scales[:, 4 * q : 4 * q + 4, :].bitcast(I32),
+            )
+        word_win.append(load_words(1))
+        nc.sync.dma_start(iss_t[:], iss)
+        raw2 = load_w_whole(w2, "raw2")
+        raw1 = load_w_whole(w1, "raw1")
+        nc.sync.dma_start(out=rows[0:CHUNKS, :], in_=time[0].rearrange("(c n) -> c n", n=CHUNK))
+        nc.sync.dma_start(out=rows[CHUNKS : 2 * CHUNKS, :], in_=cash[0].rearrange("(c n) -> c n", n=CHUNK))
 
-        rows_t = bank(0, P, "rows_t")
-        nc.tensor.transpose(rows_t[:], rows[:], ident[:])
-        cols = sb.tile([P, 2 * BLOCKS], F32, name="cols")
-        nc.vector.tensor_copy(out=cols[:], in_=rows_t[:, TIME_ROW : TIME_ROW + 2 * BLOCKS])
         neg_lam = sb.tile([P, 1], F32, name="neg_lam")
-        nc.vector.tensor_scalar(out=neg_lam[:], in0=rows_t[:, LAM_ROW : LAM_ROW + 1], scalar1=-1.0, scalar2=None, op0=ALU.mult)
-        recips = sb.tile([P, BLOCKS + 1], F32, name="recips")
-        nc.vector.reciprocal(out=recips[:], in_=rows_t[:, LAM_ROW : LAM_ROW + BLOCKS + 1])
+        nc.vector.tensor_scalar(out=neg_lam[:], in0=lam_col[:], scalar1=-1.0, scalar2=None, op0=ALU.mult)
+        recips = sb.tile([P, 2, 4], F32, name="recips")
+        nc.vector.reciprocal(out=recips[:], in_=small[:])
+        inv_lam = sb.tile([P, 1], F32, name="inv_lam")
+        nc.vector.reciprocal(out=inv_lam[:], in_=lam_col[:])
         kappa = sb.tile([P, 1], F32, name="kappa")
-        nc.vector.tensor_scalar(out=kappa[:], in0=recips[:, 0:1], scalar1=0.3, scalar2=None, op0=ALU.mult)
+        nc.vector.tensor_scalar(out=kappa[:], in0=inv_lam[:], scalar1=0.3, scalar2=None, op0=ALU.mult)
+
+        def runs(tile):
+            return tile[:].rearrange("q (p j) -> q p j", j=4)
+
+        def by_payment(wide):
+            return wide[:].rearrange("q (j p) -> q p j", j=4)
 
         def spread(src, h, bank_i, name):
             wide = bank(bank_i, BANK, name)
             for b in range(4):
-                col = 4 * h + b
-                nc.tensor.transpose(wide[:, P * b : P * (b + 1)], src[:, col : col + 1].to_broadcast([P, P]), ident[:])
+                nc.tensor.transpose(wide[:, P * b : P * (b + 1)], src[:, h, b : b + 1].to_broadcast([P, P]), ident[:])
             return wide
 
-        decay = sb.tile([P, R], F32, name="decay")
-        load = sb.tile([P, R], F32, name="load")
-        inv_wide = []
-        for h in range(2):
-            t_wide = spread(cols[:], h, 1 + h, "t_wide%d" % h)
-            nc.scalar.activation(out=decay[:, BANK * h : BANK * (h + 1)], in_=t_wide[:], func=ACT.Exp, scale=neg_lam[:])
-        for h in range(2):
-            inv_wide.append(spread(recips[:, 1:], h, 3 + h, "inv_wide%d" % h))
+        def time_factors(h, load_tag):
+            t_wide = spread(small, h, 1 + h, "t_wide%d" % h)
+            inv_wide = spread(recips, h, 3 + h, "inv_wide%d" % h)
+            decay = sb.tile([P, HALF], F32, name="decay%d" % h)
+            nc.scalar.activation(out=runs(decay), in_=by_payment(t_wide), func=ACT.Exp, scale=neg_lam[:])
+            load = sb.tile([P, HALF], F32, name="load%d" % h, tag=load_tag, align_bytes=64)
+            nc.vector.scalar_tensor_tensor(
+                out=runs(load), in0=runs(decay), scalar=1.0, in1=by_payment(inv_wide), op0=ALU.subtract, op1=ALU.mult
+            )
+            return decay, load
 
-        def quantise(raw, copies, name, split):
-            grouped = sb.tile([P, PASSES, M, PACK], BF16, name=name + "_bf", align_bytes=64)
+        decay0, load0 = time_factors(0, "load0")
+
+        def quantise(raw, copies, name):
+            grouped = sb.tile([P, PASSES, M, PACK], BF16, name=name + "_bf", tag=name + "_bf", align_bytes=64)
             codes = sb.tile([P, PASSES * M], U32, name=name + "_codes", align_bytes=64)
             scales = sb.tile([P, PASSES * M], U8, name=name + "_scales", align_bytes=64)
             for g in range(PASSES):
                 interleave(copies[g], grouped[:, g, :, :], raw[g])
-                if split:
-                    nc.vector.quantize_mx(
-                        out=codes[:, M * g : M * (g + 1)].bitcast(FP8X4),
-                        scales=scales[:, M * g : M * (g + 1)],
-                        in_=grouped[:, g, :, :].rearrange("p m j -> p (m j)"),
-                    )
-            if not split:
-                nc.vector.quantize_mx(
-                    out=codes[:].bitcast(FP8X4), scales=scales[:], in_=grouped[:].rearrange("p g m j -> p (g m j)")
-                )
+            nc.vector.quantize_mx(
+                out=codes[:].bitcast(FP8X4), scales=scales[:], in_=grouped[:].rearrange("p g m j -> p (g m j)")
+            )
             return codes, scales
 
-        q1 = quantise(raw1, [nc.vector.tensor_copy] * 2, "w1", False)
+        q3 = quantise(raw3, [nc.scalar.copy] * 2, "w3")
 
-        x_scale = sb.tile([P, S], U8, name="x_scale", align_bytes=64)
-        nc.vector.tensor_copy(x_scale[:], scale_win[:].indirect(offs_t[:]))
-        x_code = []
-        for g in range(PASSES):
+        def pick_words(g):
             picked = sb.tile([P, S], U32, name="x_code%d" % g, align_bytes=64)
             nc.vector.tensor_copy(picked[:], word_win[g][:].indirect(offs_t[:]))
-            x_code.append(picked)
+            return picked
+
+        x_code = [pick_words(0)]
+        x_scale = sb.tile([P, S], U8, name="x_scale", align_bytes=64)
+        nc.vector.tensor_copy(x_scale[:], scale_win[:].indirect(offs_t[:]))
+        x_code.append(pick_words(1))
+        decay1, load1 = time_factors(1, "word_win1")
+        decay, load = (decay0, decay1), (load0, load1)
 
         def product(q, bank_i, name):
             codes, scales = q
@@ -169,60 +169,92 @@ def tile_picked_ynels_price_p_kernel(
                 )
             return acc
 
-        yl = product(q1, 5, "yl")
-        nc.scalar.activation(out=level[:, 0:S], in_=yl[:], func=ACT.Copy, scale=-0.15, bias=-0.225)
-
-        for h in range(2):
-            half = slice(BANK * h, BANK * (h + 1))
-            nc.vector.scalar_tensor_tensor(
-                out=load[:, half], in0=decay[:, half], scalar=1.0, in1=inv_wide[h][:], op0=ALU.subtract, op1=ALU.mult
-            )
-
-        def offsets(c):
-            return iss_t[:, (CHUNK // 16) * c : (CHUNK // 16) * (c + 1)]
-
-        term_l = []
-        for c in range(CHUNKS):
-            term = sb.tile([P, CHUNK], F32, name="term_l%d" % c)
-            nc.vector.tensor_copy(term[:], level[:].indirect(offsets(c)))
-            term_l.append(term)
-
-        q3 = quantise(raw3, [nc.scalar.copy] * 2, "w3", False)
-        yh = product(q3, 6, "yh")
+        yh = product(q3, 5, "yh")
         nc.scalar.activation(out=hump[:, 0:S], in_=yh[:], func=ACT.Copy, scale=0.3)
+
+        def looked_up(table, first, count, other, op, name, tag):
+            term = sb.tile([P, count], F32, name=name, tag=tag, align_bytes=64)
+            window = table[:].indirect(iss_t[:, first // 16 : (first + count) // 16])
+            nc.vector.tensor_tensor(term[:], window, other, op)
+            return term
+
+        def half_term(table, factor, h, name, tag):
+            return looked_up(table, HALF * h, HALF, factor[h][:], ALU.mult, name, tag)
+
+        term_h = [half_term(hump, decay, 0, "term_h0", "term_h0")]
+        q2 = quantise(raw2, [nc.scalar.copy] * 2, "w2")
         hump_k = sb.tile([P, S], F32, name="hump_k")
         nc.scalar.activation(out=hump_k[:], in_=yh[:], func=ACT.Copy, scale=kappa[:])
-
-        raw2 = [load_w(w2, g, "raw2_%d" % g, ("rows", "raw1")[g])[:] for g in range(PASSES)]
-        q2 = quantise(raw2, [nc.scalar.copy] * 2, "w2", True)
-        ys = product(q2, 7, "ys")
+        ys = product(q2, 6, "ys")
+        term_h.append(half_term(hump, decay, 1, "term_h1", "w2_bf"))
+        q1 = quantise(raw1, [nc.scalar.copy] * 2, "w1")
+        yl = product(q1, 7, "yl")
+        nc.scalar.activation(out=level[:, 0:S], in_=yl[:], func=ACT.Copy, scale=-0.15, bias=-0.225)
         nc.vector.scalar_tensor_tensor(
             out=slope[:, 0:S], in0=ys[:], scalar=kappa[:], in1=hump_k[:], op0=ALU.mult, op1=ALU.add
         )
 
-        for c in range(CHUNKS):
-            span = slice(CHUNK * c, CHUNK * (c + 1))
-            term_h = sb.tile([P, CHUNK], F32, name="term_h%d" % c)
-            nc.vector.tensor_tensor(term_h[:], hump[:].indirect(offsets(c)), decay[:, span], ALU.mult)
-            term_s = sb.tile([P, CHUNK], F32, name="term_s%d" % c)
-            nc.vector.tensor_tensor(term_s[:], slope[:].indirect(offsets(c)), load[:, span], ALU.mult)
-            back = bank(4 + c % 2, CHUNK, "back%d" % c)
-            for i in range(CHUNK // P):
-                b = c * (CHUNK // P) + i
-                part = slice(P * i, P * (i + 1))
-                total = bank(b % 4, P, "total%d" % b)
-                terms = (term_l[c], term_h, term_s)
-                for n, term in enumerate(terms):
-                    nc.tensor.matmul(
-                        total[:], lhsT=term[:, part], rhs=ident[:], start=(n == 0), stop=(n == len(terms) - 1), is_transpose=True
-                    )
-                disc = sb.tile([P, P], F32, name="disc%d" % b)
-                nc.scalar.activation(out=disc[:], in_=total[:], func=ACT.Exp, scale=cols[:, b : b + 1])
-                value = sb.tile([P, P], F32, name="value%d" % b)
-                nc.scalar.activation(out=value[:], in_=disc[:], func=ACT.Copy, scale=cols[:, BLOCKS + b : BLOCKS + b + 1])
-                nc.tensor.transpose(back[:, part], value[:], ident[:])
-            price = sb.tile([P, CHUNK // D], F32, name="price%d" % c)
+        rows_t = bank(0, 2 * P, "rows_t")
+        for e in range(2):
+            nc.tensor.transpose(rows_t[:, P * e : P * (e + 1)], rows[:, e::2], ident[:])
+        cols = sb.tile([P, 2, 2 * CHUNKS], F32, name="cols")
+        nc.scalar.copy(out=cols[:], in_=rows_t[:].rearrange("p (e n) -> p e n", e=2)[:, :, 0 : 2 * CHUNKS])
+
+        def turn(target, source, first):
+            nc.tensor.matmul(target, lhsT=source, rhs=ident[:], start=first, stop=not first, is_transpose=True)
+
+        totals = {}
+
+        def open_sums(h, slope_tag):
+            term_s = half_term(slope, load, h, "term_s%d" % h, slope_tag)
+            for c in (2 * h, 2 * h + 1):
+                for e in range(2):
+                    totals[c, e] = bank(2 * c + e, P, "total%d_%d" % (c, e))
+                    first = CHUNK * (c % 2)
+                    turn(totals[c, e][:], term_s[:, first + e : first + CHUNK : 2], True)
+
+        def discount(c):
+            other = term_h[c // 2][:, CHUNK * (c % 2) : CHUNK * (c % 2 + 1)]
+            term_l = looked_up(level, CHUNK * c, CHUNK, other, ALU.add, "term_l%d" % c, "term_l%d" % c)
+            discs = []
+            for e in range(2):
+                turn(totals[c, e][:], term_l[:, e::2], False)
+                disc = sb.tile([P, P], F32, name="disc%d_%d" % (c, e))
+                nc.scalar.activation(out=disc[:], in_=totals[c, e][:], func=ACT.Exp, scale=cols[:, e, c : c + 1])
+                discs.append(disc)
+            return discs
+
+        def turn_back(c, discs, on_vector):
+            back = bank(c, P, "back%d" % c)
+            for e, disc in enumerate(discs):
+                value = sb.tile([P, P], F32, name="value%d_%d" % (c, e))
+                payment = cols[:, e, CHUNKS + c : CHUNKS + c + 1]
+                if on_vector:
+                    nc.vector.tensor_scalar(out=value[:], in0=disc[:], scalar1=payment, scalar2=None, op0=ALU.mult)
+                else:
+                    nc.scalar.activation(out=value[:], in_=disc[:], func=ACT.Copy, scale=payment)
+                turn(back[:], value[:], e == 0)
+            return back
+
+        def store(c, back):
+            bonds = CHUNK // D
+            price = sb.tile([P, bonds], F32, name="price%d" % c)
             nc.vector.tensor_reduce(
-                out=price[:], in_=back[:].rearrange("p (v d) -> p v d", d=D), axis=mybir.AxisListType.X, op=ALU.add
+                out=price[:], in_=back[:].rearrange("p (v d) -> p v d", d=2), axis=mybir.AxisListType.X, op=ALU.add
             )
-            nc.sync.dma_start(out=out[:, (CHUNK // D) * c : (CHUNK // D) * (c + 1)], in_=price[:])
+            nc.sync.dma_start(out=out[:, bonds * c : bonds * (c + 1)], in_=price[:])
+
+        open_sums(0, "w1_bf")
+        discs0 = discount(0)
+        discs1 = discount(1)
+        back0 = turn_back(0, discs0, False)
+        open_sums(1, "term_s1")
+        back1 = turn_back(1, discs1, False)
+        discs2 = discount(2)
+        discs3 = discount(3)
+        store(0, back0)
+        store(1, back1)
+        back2 = turn_back(2, discs2, True)
+        back3 = turn_back(3, discs3, True)
+        store(2, back2)
+        store(3, back3)

@@ -19,20 +19,13 @@ ACT = mybir.ActivationFunctionType
 P = 128
 PACK = 4
 PASSES = K // (P * PACK)
-BANK = 512
-BLOCKS = R // P
-CHUNK = 256
-CHUNKS = R // CHUNK
+LIST_ROWS = 16
+QUADRANT = 32
 HALF = 512
+RUN = HALF // P
+CHUNK = 2 * P
+CHUNKS = R // CHUNK
 SPARE = 16
-RUN = R // P
-
-
-def interleave(engine_copy, grouped, raw):
-    engine_copy(
-        out=grouped.rearrange("p (c i) j -> p c j i", i=4),
-        in_=raw.rearrange("p j (c i) -> p c j i", i=4),
-    )
 
 
 def tile_picked_ynels_price_p_kernel(
@@ -57,141 +50,143 @@ def tile_picked_ynels_price_p_kernel(
         nc.vector.memset(slope[:, S:], 0.0)
         rows = sb.tile([P, CHUNK], F32, name="rows")
         nc.vector.memset(rows[:], 0.0)
-
         nc.scalar.activation(out=level[:, S:], in_=hump[:, S : S + SPARE], func=ACT.Exp)
 
-        offs_t = sb.tile([P, S // 16], U16, name="offs_t")
-        iss_t = sb.tile([P, R // 16], U16, name="iss_t")
+        offs_t = sb.tile([P, S // LIST_ROWS], U16, name="offs_t")
+        iss_t = sb.tile([P, R // LIST_ROWS], U16, name="iss_t")
 
-        def load_w_whole(w, name):
+        def load_weight(w, name):
             raw = sb.tile([P, PASSES, PACK, M], F32, name=name)
             nc.sync.dma_start(
                 out=raw[:].rearrange("p g j m -> p g (j m)"),
                 in_=w.rearrange("(g p j) m -> p g (j m)", g=PASSES, j=PACK),
             )
-            return [raw[:, g, :, :] for g in range(PASSES)]
+            return raw
 
-        small = sb.tile([P, 2, 4], F32, name="small")
-        nc.sync.dma_start(out=small[:], in_=time[0].rearrange("(h p j) -> p h j", h=2, j=4))
-        nc.sync.dma_start(offs_t[:], offs)
-        raw3 = load_w_whole(w3, "raw3")
-        lam_col = sb.tile([P, 1], F32, name="lam_col")
-        nc.sync.dma_start(out=lam_col[:], in_=lam)
         def load_words(g):
             win = sb.tile([P, T], U32, name="word_win%d" % g, tag="word_win%d" % g, align_bytes=64)
             nc.sync.dma_start(out=win[:].bitcast(I32), in_=x_words[g].rearrange("p n t -> p (n t)").bitcast(I32))
             return win
 
-        word_win = [load_words(0)]
-        for q in range(4):
+        time_runs = sb.tile([P, R // HALF, RUN], F32, name="time_runs")
+        nc.sync.dma_start(out=time_runs[:], in_=time[0].rearrange("(h p j) -> p h j", h=R // HALF, j=RUN))
+        nc.sync.dma_start(offs_t[:], offs)
+        raw3 = load_weight(w3, "raw3")
+        lam_col = sb.tile([P, 1], F32, name="lam_col")
+        nc.sync.dma_start(out=lam_col[:], in_=lam)
+        for q in range(P // QUADRANT):
             nc.sync.dma_start(
-                out=scale_win[32 * q : 32 * q + 4 * PASSES, :].bitcast(I32),
+                out=scale_win[QUADRANT * q : QUADRANT * q + 4 * PASSES, :].bitcast(I32),
                 in_=x_scales[:, 4 * q : 4 * q + 4, :].bitcast(I32),
             )
-        word_win.append(load_words(1))
+        word_win = [load_words(g) for g in range(PASSES)]
         nc.sync.dma_start(iss_t[:], iss)
-        raw2 = load_w_whole(w2, "raw2")
-        raw1 = load_w_whole(w1, "raw1")
+        raw2 = load_weight(w2, "raw2")
+        raw1 = load_weight(w1, "raw1")
         nc.sync.dma_start(out=rows[0:CHUNKS, :], in_=time[0].rearrange("(c n) -> c n", n=CHUNK))
         nc.sync.dma_start(out=rows[CHUNKS : 2 * CHUNKS, :], in_=cash[0].rearrange("(c n) -> c n", n=CHUNK))
 
         neg_lam = sb.tile([P, 1], F32, name="neg_lam")
         nc.vector.tensor_scalar(out=neg_lam[:], in0=lam_col[:], scalar1=-1.0, scalar2=None, op0=ALU.mult)
-        recips = sb.tile([P, 2, 4], F32, name="recips")
-        nc.vector.reciprocal(out=recips[:], in_=small[:])
+        inv_time_runs = sb.tile([P, R // HALF, RUN], F32, name="inv_time_runs")
+        nc.vector.reciprocal(out=inv_time_runs[:], in_=time_runs[:])
         inv_lam = sb.tile([P, 1], F32, name="inv_lam")
         nc.vector.reciprocal(out=inv_lam[:], in_=lam_col[:])
-        kappa = sb.tile([P, 1], F32, name="kappa")
-        nc.vector.tensor_scalar(out=kappa[:], in0=inv_lam[:], scalar1=0.3, scalar2=None, op0=ALU.mult)
+        slope_gain = sb.tile([P, 1], F32, name="slope_gain")
+        nc.vector.tensor_scalar(out=slope_gain[:], in0=inv_lam[:], scalar1=0.3, scalar2=None, op0=ALU.mult)
 
-        def runs(tile):
-            return tile[:].rearrange("q (p j) -> q p j", j=4)
+        def spread(runs, h, bank_i, name):
+            wide = bank(bank_i, HALF, name)
+            for j in range(RUN):
+                nc.tensor.transpose(wide[:, P * j : P * (j + 1)], runs[:, h, j : j + 1].to_broadcast([P, P]), ident[:])
+            return wide[:].rearrange("q (j p) -> q p j", j=RUN)
 
-        def by_payment(wide):
-            return wide[:].rearrange("q (j p) -> q p j", j=4)
+        def in_runs(tile):
+            return tile[:].rearrange("q (p j) -> q p j", j=RUN)
 
-        def spread(src, h, bank_i, name):
-            wide = bank(bank_i, BANK, name)
-            for b in range(4):
-                nc.tensor.transpose(wide[:, P * b : P * (b + 1)], src[:, h, b : b + 1].to_broadcast([P, P]), ident[:])
-            return wide
-
-        def time_factors(h, load_tag):
-            t_wide = spread(small, h, 1 + h, "t_wide%d" % h)
-            inv_wide = spread(recips, h, 3 + h, "inv_wide%d" % h)
-            decay = sb.tile([P, HALF], F32, name="decay%d" % h)
-            nc.scalar.activation(out=runs(decay), in_=by_payment(t_wide), func=ACT.Exp, scale=neg_lam[:])
-            load = sb.tile([P, HALF], F32, name="load%d" % h, tag=load_tag, align_bytes=64)
+        def time_factors(h, loading_tag):
+            time_wide = spread(time_runs, h, 1 + h, "time_wide%d" % h)
+            inv_time_wide = spread(inv_time_runs, h, 3 + h, "inv_time_wide%d" % h)
+            decay_h = sb.tile([P, HALF], F32, name="decay%d" % h)
+            nc.scalar.activation(out=in_runs(decay_h), in_=time_wide, func=ACT.Exp, scale=neg_lam[:])
+            loading_h = sb.tile([P, HALF], F32, name="loading%d" % h, tag=loading_tag, align_bytes=64)
             nc.vector.scalar_tensor_tensor(
-                out=runs(load), in0=runs(decay), scalar=1.0, in1=by_payment(inv_wide), op0=ALU.subtract, op1=ALU.mult
+                out=in_runs(loading_h), in0=in_runs(decay_h), scalar=1.0, in1=inv_time_wide, op0=ALU.subtract, op1=ALU.mult
             )
-            return decay, load
+            return decay_h, loading_h
 
-        decay0, load0 = time_factors(0, "load0")
+        decay0, loading0 = time_factors(0, "loading0")
 
-        def quantise(raw, copies, name):
+        def quantise(raw, name):
             grouped = sb.tile([P, PASSES, M, PACK], BF16, name=name + "_bf", tag=name + "_bf", align_bytes=64)
             codes = sb.tile([P, PASSES * M], U32, name=name + "_codes", align_bytes=64)
             scales = sb.tile([P, PASSES * M], U8, name=name + "_scales", align_bytes=64)
             for g in range(PASSES):
-                interleave(copies[g], grouped[:, g, :, :], raw[g])
+                nc.scalar.copy(
+                    out=grouped[:, g, :, :].rearrange("p (c i) j -> p c j i", i=4),
+                    in_=raw[:, g, :, :].rearrange("p j (c i) -> p c j i", i=4),
+                )
             nc.vector.quantize_mx(
                 out=codes[:].bitcast(FP8X4), scales=scales[:], in_=grouped[:].rearrange("p g m j -> p (g m j)")
             )
             return codes, scales
 
-        q3 = quantise(raw3, [nc.scalar.copy] * 2, "w3")
+        mx3 = quantise(raw3, "w3")
 
-        def pick_words(g):
+        def pick_words(g, pieces):
             picked = sb.tile([P, S], U32, name="x_code%d" % g, align_bytes=64)
-            nc.vector.tensor_copy(picked[:], word_win[g][:].indirect(offs_t[:]))
+            width = S // pieces
+            for i in range(pieces):
+                offsets = offs_t[:, width // LIST_ROWS * i : width // LIST_ROWS * (i + 1)]
+                nc.vector.tensor_copy(picked[:, width * i : width * (i + 1)], word_win[g][:].indirect(offsets))
             return picked
 
-        x_code = [pick_words(0)]
         x_scale = sb.tile([P, S], U8, name="x_scale", align_bytes=64)
         nc.vector.tensor_copy(x_scale[:], scale_win[:].indirect(offs_t[:]))
-        x_code.append(pick_words(1))
-        decay1, load1 = time_factors(1, "word_win1")
-        decay, load = (decay0, decay1), (load0, load1)
+        x_code = [pick_words(0, 1), pick_words(1, 2)]
+        decay1, loading1 = time_factors(1, "word_win1")
+        decay, loading = (decay0, decay1), (loading0, loading1)
 
-        def product(q, bank_i, name):
-            codes, scales = q
-            acc = bank(bank_i, S, name)
+        def product(mx, bank_i, name, issuers=slice(0, S)):
+            codes, scales = mx
+            acc = bank(bank_i, issuers.stop - issuers.start, name)
             for g in range(PASSES):
                 nc.tensor.matmul_mx(
                     out=acc[:],
                     lhsT=codes[:, M * g : M * (g + 1)].bitcast(FP8X4),
                     lhsT_scale=scales[:, M * g : M * (g + 1)],
-                    rhs=x_code[g][:].bitcast(FP8X4),
-                    rhs_scale=x_scale[4 * g : P, :],
+                    rhs=x_code[g][:, issuers].bitcast(FP8X4),
+                    rhs_scale=x_scale[4 * g : P, issuers],
                     start=(g == 0),
                     stop=(g == PASSES - 1),
                 )
             return acc
 
-        yh = product(q3, 5, "yh")
-        nc.scalar.activation(out=hump[:, 0:S], in_=yh[:], func=ACT.Copy, scale=0.3)
+        for i, bank_i in enumerate((0, 5)):
+            issuers = slice(S // 2 * i, S // 2 * (i + 1))
+            yh = product(mx3, bank_i, "yh%d" % i, issuers)
+            nc.scalar.activation(out=hump[:, issuers], in_=yh[:], func=ACT.Copy, scale=0.3)
 
         def looked_up(table, first, count, other, op, name, tag):
             term = sb.tile([P, count], F32, name=name, tag=tag, align_bytes=64)
-            window = table[:].indirect(iss_t[:, first // 16 : (first + count) // 16])
-            nc.vector.tensor_tensor(term[:], window, other, op)
+            offsets = iss_t[:, first // LIST_ROWS : (first + count) // LIST_ROWS]
+            nc.vector.tensor_tensor(term[:], table[:].indirect(offsets), other, op)
             return term
 
         def half_term(table, factor, h, name, tag):
             return looked_up(table, HALF * h, HALF, factor[h][:], ALU.mult, name, tag)
 
         term_h = [half_term(hump, decay, 0, "term_h0", "term_h0")]
-        q2 = quantise(raw2, [nc.scalar.copy] * 2, "w2")
-        hump_k = sb.tile([P, S], F32, name="hump_k")
-        nc.scalar.activation(out=hump_k[:], in_=yh[:], func=ACT.Copy, scale=kappa[:])
-        ys = product(q2, 6, "ys")
+        mx2 = quantise(raw2, "w2")
+        hump_over_lam = sb.tile([P, S], F32, name="hump_over_lam")
+        nc.scalar.activation(out=hump_over_lam[:], in_=hump[:, 0:S], func=ACT.Copy, scale=inv_lam[:])
+        ys = product(mx2, 6, "ys")
         term_h.append(half_term(hump, decay, 1, "term_h1", "w2_bf"))
-        q1 = quantise(raw1, [nc.scalar.copy] * 2, "w1")
-        yl = product(q1, 7, "yl")
+        mx1 = quantise(raw1, "w1")
+        yl = product(mx1, 7, "yl")
         nc.scalar.activation(out=level[:, 0:S], in_=yl[:], func=ACT.Copy, scale=-0.15, bias=-0.225)
         nc.vector.scalar_tensor_tensor(
-            out=slope[:, 0:S], in0=ys[:], scalar=kappa[:], in1=hump_k[:], op0=ALU.mult, op1=ALU.add
+            out=slope[:, 0:S], in0=ys[:], scalar=slope_gain[:], in1=hump_over_lam[:], op0=ALU.mult, op1=ALU.add
         )
 
         rows_t = bank(0, 2 * P, "rows_t")
@@ -205,8 +200,8 @@ def tile_picked_ynels_price_p_kernel(
 
         totals = {}
 
-        def open_sums(h, slope_tag):
-            term_s = half_term(slope, load, h, "term_s%d" % h, slope_tag)
+        def open_sums(h, term_tag):
+            term_s = half_term(slope, loading, h, "term_s%d" % h, term_tag)
             for c in (2 * h, 2 * h + 1):
                 for e in range(2):
                     totals[c, e] = bank(2 * c + e, P, "total%d_%d" % (c, e))
@@ -224,15 +219,17 @@ def tile_picked_ynels_price_p_kernel(
                 discs.append(disc)
             return discs
 
-        def turn_back(c, discs, on_vector):
+        def times_cash_on_scalar(value, disc, payment):
+            nc.scalar.activation(out=value, in_=disc, func=ACT.Copy, scale=payment)
+
+        def times_cash_on_vector(value, disc, payment):
+            nc.vector.tensor_scalar(out=value, in0=disc, scalar1=payment, scalar2=None, op0=ALU.mult)
+
+        def turn_back(c, discs, times_cash):
             back = bank(c, P, "back%d" % c)
             for e, disc in enumerate(discs):
                 value = sb.tile([P, P], F32, name="value%d_%d" % (c, e))
-                payment = cols[:, e, CHUNKS + c : CHUNKS + c + 1]
-                if on_vector:
-                    nc.vector.tensor_scalar(out=value[:], in0=disc[:], scalar1=payment, scalar2=None, op0=ALU.mult)
-                else:
-                    nc.scalar.activation(out=value[:], in_=disc[:], func=ACT.Copy, scale=payment)
+                times_cash(value[:], disc[:], cols[:, e, CHUNKS + c : CHUNKS + c + 1])
                 turn(back[:], value[:], e == 0)
             return back
 
@@ -247,14 +244,14 @@ def tile_picked_ynels_price_p_kernel(
         open_sums(0, "w1_bf")
         discs0 = discount(0)
         discs1 = discount(1)
-        back0 = turn_back(0, discs0, False)
+        back0 = turn_back(0, discs0, times_cash_on_scalar)
         open_sums(1, "term_s1")
-        back1 = turn_back(1, discs1, False)
+        back1 = turn_back(1, discs1, times_cash_on_scalar)
         discs2 = discount(2)
         discs3 = discount(3)
         store(0, back0)
         store(1, back1)
-        back2 = turn_back(2, discs2, True)
-        back3 = turn_back(3, discs3, True)
+        back2 = turn_back(2, discs2, times_cash_on_vector)
+        back3 = turn_back(3, discs3, times_cash_on_vector)
         store(2, back2)
         store(3, back3)

from contextlib import ExitStack

import concourse.mybir as mybir
from concourse.masks import make_identity

K, T, S, M, R, D = 1024, 1024, 256, 128, 1024, 4
FLOPS = 3 * 2 * K * M * S

F32 = mybir.dt.float32
BF16 = mybir.dt.bfloat16
I32 = mybir.dt.int32
U32 = mybir.dt.uint32
U16 = mybir.dt.uint16
U8 = mybir.dt.uint8
FP8X4 = mybir.dt.float8_e4m3fn_x4
ALU = mybir.AluOpType
ACT = mybir.ActivationFunctionType

P = 128
PACK = 4
PASSES = K // (P * PACK)
LIST_ROWS = 16
QUADRANT = 32
HALF = 512
RUN = HALF // P
CHUNK = 2 * P
CHUNKS = R // CHUNK
SPARE = 16


def tile_picked_ynels_price_p_kernel(
    tc, x_words, x_scales, w1, w2, w3, time, lam, cash, offs, iss, out
):
    nc = tc.nc
    with ExitStack() as ctx:
        sb = ctx.enter_context(tc.tile_pool(name="sb", bufs=1))
        ps = ctx.enter_context(tc.psum_pool(name="ps", bufs=1))

        def bank(i, cols, name):
            return ps.tile([P, cols], F32, name=name, tag="bank%d" % i)

        scale_win = sb.tile([P, T], U8, name="scale_win", align_bytes=64)
        nc.gpsimd.memset(scale_win[:].bitcast(I32), 0)
        ident = sb.tile([P, P], F32, name="ident")
        make_identity(nc, ident[:])
        level = sb.tile([P, CHUNK + SPARE], F32, name="level")
        hump = sb.tile([P, HALF + SPARE], F32, name="hump")
        slope = sb.tile([P, HALF + SPARE], F32, name="slope")
        nc.vector.memset(hump[:, S:], 0.0)
        nc.vector.memset(slope[:, S:], 0.0)
        rows = sb.tile([P, CHUNK], F32, name="rows")
        nc.vector.memset(rows[:], 0.0)
        nc.scalar.activation(out=level[:, S:], in_=hump[:, S : S + SPARE], func=ACT.Exp)

        offs_t = sb.tile([P, S // LIST_ROWS], U16, name="offs_t")
        iss_t = sb.tile([P, R // LIST_ROWS], U16, name="iss_t")

        def load_weight(w, name):
            raw = sb.tile([P, PASSES, PACK, M], F32, name=name)
            nc.sync.dma_start(
                out=raw[:].rearrange("p g j m -> p g (j m)"),
                in_=w.rearrange("(g p j) m -> p g (j m)", g=PASSES, j=PACK),
            )
            return raw

        def load_words(g):
            win = sb.tile([P, T], U32, name="word_win%d" % g, tag="word_win%d" % g, align_bytes=64)
            nc.sync.dma_start(out=win[:].bitcast(I32), in_=x_words[g].rearrange("p n t -> p (n t)").bitcast(I32))
            return win

        time_runs = sb.tile([P, R // HALF, RUN], F32, name="time_runs")
        nc.sync.dma_start(out=time_runs[:], in_=time[0].rearrange("(h p j) -> p h j", h=R // HALF, j=RUN))
        nc.sync.dma_start(offs_t[:], offs)
        raw3 = load_weight(w3, "raw3")
        lam_col = sb.tile([P, 1], F32, name="lam_col")
        nc.sync.dma_start(out=lam_col[:], in_=lam)
        for q in range(P // QUADRANT):
            nc.sync.dma_start(
                out=scale_win[QUADRANT * q : QUADRANT * q + 4 * PASSES, :].bitcast(I32),
                in_=x_scales[:, 4 * q : 4 * q + 4, :].bitcast(I32),
            )
        word_win = [load_words(g) for g in range(PASSES)]
        nc.sync.dma_start(iss_t[:], iss)
        raw2 = load_weight(w2, "raw2")
        raw1 = load_weight(w1, "raw1")
        nc.sync.dma_start(out=rows[0:CHUNKS, :], in_=time[0].rearrange("(c n) -> c n", n=CHUNK))
        nc.sync.dma_start(out=rows[CHUNKS : 2 * CHUNKS, :], in_=cash[0].rearrange("(c n) -> c n", n=CHUNK))

        neg_lam = sb.tile([P, 1], F32, name="neg_lam")
        nc.vector.tensor_scalar(out=neg_lam[:], in0=lam_col[:], scalar1=-1.0, scalar2=None, op0=ALU.mult)
        inv_time_runs = sb.tile([P, R // HALF, RUN], F32, name="inv_time_runs")
        nc.vector.reciprocal(out=inv_time_runs[:], in_=time_runs[:])
        inv_lam = sb.tile([P, 1], F32, name="inv_lam")
        nc.vector.reciprocal(out=inv_lam[:], in_=lam_col[:])
        slope_gain = sb.tile([P, 1], F32, name="slope_gain")
        nc.vector.tensor_scalar(out=slope_gain[:], in0=inv_lam[:], scalar1=0.3, scalar2=None, op0=ALU.mult)

        def spread(runs, h, bank_i, name):
            wide = bank(bank_i, HALF, name)
            for j in range(RUN):
                nc.tensor.transpose(wide[:, P * j : P * (j + 1)], runs[:, h, j : j + 1].to_broadcast([P, P]), ident[:])
            return wide[:].rearrange("q (j p) -> q p j", j=RUN)

        def in_runs(tile):
            return tile[:].rearrange("q (p j) -> q p j", j=RUN)

        def time_factors(h, loading_tag):
            time_wide = spread(time_runs, h, 1 + h, "time_wide%d" % h)
            inv_time_wide = spread(inv_time_runs, h, 3 + h, "inv_time_wide%d" % h)
            decay_h = sb.tile([P, HALF], F32, name="decay%d" % h)
            nc.scalar.activation(out=in_runs(decay_h), in_=time_wide, func=ACT.Exp, scale=neg_lam[:])
            loading_h = sb.tile([P, HALF], F32, name="loading%d" % h, tag=loading_tag, align_bytes=64)
            nc.vector.scalar_tensor_tensor(
                out=in_runs(loading_h), in0=in_runs(decay_h), scalar=1.0, in1=inv_time_wide, op0=ALU.subtract, op1=ALU.mult
            )
            return decay_h, loading_h

        decay0, loading0 = time_factors(0, "loading0")

        def quantise(raw, name):
            grouped = sb.tile([P, PASSES, M, PACK], BF16, name=name + "_bf", tag=name + "_bf", align_bytes=64)
            codes = sb.tile([P, PASSES * M], U32, name=name + "_codes", align_bytes=64)
            scales = sb.tile([P, PASSES * M], U8, name=name + "_scales", align_bytes=64)
            for g in range(PASSES):
                nc.scalar.copy(
                    out=grouped[:, g, :, :].rearrange("p (c i) j -> p c j i", i=4),
                    in_=raw[:, g, :, :].rearrange("p j (c i) -> p c j i", i=4),
                )
            nc.vector.quantize_mx(
                out=codes[:].bitcast(FP8X4), scales=scales[:], in_=grouped[:].rearrange("p g m j -> p (g m j)")
            )
            return codes, scales

        mx3 = quantise(raw3, "w3")

        def pick_words(g, pieces):
            picked = sb.tile([P, S], U32, name="x_code%d" % g, align_bytes=64)
            width = S // pieces
            for i in range(pieces):
                offsets = offs_t[:, width // LIST_ROWS * i : width // LIST_ROWS * (i + 1)]
                nc.vector.tensor_copy(picked[:, width * i : width * (i + 1)], word_win[g][:].indirect(offsets))
            return picked

        x_scale = sb.tile([P, S], U8, name="x_scale", align_bytes=64)
        nc.vector.tensor_copy(x_scale[:], scale_win[:].indirect(offs_t[:]))
        x_code = [pick_words(0, 1), pick_words(1, 2)]
        decay1, loading1 = time_factors(1, "word_win1")
        decay, loading = (decay0, decay1), (loading0, loading1)

        def product(mx, bank_i, name, issuers=slice(0, S)):
            codes, scales = mx
            acc = bank(bank_i, issuers.stop - issuers.start, name)
            for g in range(PASSES):
                nc.tensor.matmul_mx(
                    out=acc[:],
                    lhsT=codes[:, M * g : M * (g + 1)].bitcast(FP8X4),
                    lhsT_scale=scales[:, M * g : M * (g + 1)],
                    rhs=x_code[g][:, issuers].bitcast(FP8X4),
                    rhs_scale=x_scale[4 * g : P, issuers],
                    start=(g == 0),
                    stop=(g == PASSES - 1),
                )
            return acc

        for i, bank_i in enumerate((0, 5)):
            issuers = slice(S // 2 * i, S // 2 * (i + 1))
            yh = product(mx3, bank_i, "yh%d" % i, issuers)
            nc.scalar.activation(out=hump[:, issuers], in_=yh[:], func=ACT.Copy, scale=0.3)

        def looked_up(table, first, count, other, op, name, tag):
            term = sb.tile([P, count], F32, name=name, tag=tag, align_bytes=64)
            offsets = iss_t[:, first // LIST_ROWS : (first + count) // LIST_ROWS]
            nc.vector.tensor_tensor(term[:], table[:].indirect(offsets), other, op)
            return term

        def half_term(table, factor, h, name, tag):
            return looked_up(table, HALF * h, HALF, factor[h][:], ALU.mult, name, tag)

        term_h = [half_term(hump, decay, 0, "term_h0", "term_h0")]
        mx2 = quantise(raw2, "w2")
        hump_over_lam = sb.tile([P, S], F32, name="hump_over_lam")
        nc.scalar.activation(out=hump_over_lam[:], in_=hump[:, 0:S], func=ACT.Copy, scale=inv_lam[:])
        ys = product(mx2, 6, "ys")
        term_h.append(half_term(hump, decay, 1, "term_h1", "w2_bf"))
        mx1 = quantise(raw1, "w1")
        yl = product(mx1, 7, "yl")
        nc.scalar.activation(out=level[:, 0:S], in_=yl[:], func=ACT.Copy, scale=-0.15, bias=-0.225)
        nc.vector.scalar_tensor_tensor(
            out=slope[:, 0:S], in0=ys[:], scalar=slope_gain[:], in1=hump_over_lam[:], op0=ALU.mult, op1=ALU.add
        )

        rows_t = bank(0, 2 * P, "rows_t")
        for e in range(2):
            nc.tensor.transpose(rows_t[:, P * e : P * (e + 1)], rows[:, e::2], ident[:])
        cols = sb.tile([P, 2, 2 * CHUNKS], F32, name="cols")
        nc.scalar.copy(out=cols[:], in_=rows_t[:].rearrange("p (e n) -> p e n", e=2)[:, :, 0 : 2 * CHUNKS])

        def turn(target, source, first):
            nc.tensor.matmul(target, lhsT=source, rhs=ident[:], start=first, stop=not first, is_transpose=True)

        totals = {}

        def open_sums(h, term_tag):
            term_s = half_term(slope, loading, h, "term_s%d" % h, term_tag)
            for c in (2 * h, 2 * h + 1):
                for e in range(2):
                    totals[c, e] = bank(2 * c + e, P, "total%d_%d" % (c, e))
                    first = CHUNK * (c % 2)
                    turn(totals[c, e][:], term_s[:, first + e : first + CHUNK : 2], True)

        def discount(c):
            other = term_h[c // 2][:, CHUNK * (c % 2) : CHUNK * (c % 2 + 1)]
            term_l = looked_up(level, CHUNK * c, CHUNK, other, ALU.add, "term_l%d" % c, "term_l%d" % c)
            discs = []
            for e in range(2):
                turn(totals[c, e][:], term_l[:, e::2], False)
                disc = sb.tile([P, P], F32, name="disc%d_%d" % (c, e))
                nc.scalar.activation(out=disc[:], in_=totals[c, e][:], func=ACT.Exp, scale=cols[:, e, c : c + 1])
                discs.append(disc)
            return discs

        def times_cash_on_scalar(value, disc, payment):
            nc.scalar.activation(out=value, in_=disc, func=ACT.Copy, scale=payment)

        def times_cash_on_vector(value, disc, payment):
            nc.vector.tensor_scalar(out=value, in0=disc, scalar1=payment, scalar2=None, op0=ALU.mult)

        def turn_back(c, discs, times_cash):
            back = bank(c, P, "back%d" % c)
            for e, disc in enumerate(discs):
                value = sb.tile([P, P], F32, name="value%d_%d" % (c, e))
                times_cash(value[:], disc[:], cols[:, e, CHUNKS + c : CHUNKS + c + 1])
                turn(back[:], value[:], e == 0)
            return back

        def store(c, back):
            bonds = CHUNK // D
            price = sb.tile([P, bonds], F32, name="price%d" % c)
            nc.vector.tensor_reduce(
                out=price[:], in_=back[:].rearrange("p (v d) -> p v d", d=2), axis=mybir.AxisListType.X, op=ALU.add
            )
            nc.sync.dma_start(out=out[:, bonds * c : bonds * (c + 1)], in_=price[:])

        open_sums(0, "w1_bf")
        discs0 = discount(0)
        discs1 = discount(1)
        back0 = turn_back(0, discs0, times_cash_on_scalar)
        open_sums(1, "term_s1")
        back1 = turn_back(1, discs1, times_cash_on_scalar)
        discs2 = discount(2)
        discs3 = discount(3)
        store(0, back0)
        store(1, back1)
        back2 = turn_back(2, discs2, times_cash_on_vector)
        back3 = turn_back(3, discs3, times_cash_on_vector)
        store(2, back2)
        store(3, back3)
